import numpy as np
import ml_dtypes


def mxq(x, axis, fmt="e4m3"):
    dtype, down = {"e4m3": (ml_dtypes.float8_e4m3fn, 7), "e5m2": (ml_dtypes.float8_e5m2, 14)}[fmt]
    v = np.moveaxis(np.asarray(x, np.float32).astype(ml_dtypes.bfloat16).astype(np.float64), axis, -1)
    blocks = v.reshape(v.shape[:-1] + (-1, 32))
    amax = np.abs(blocks).max(-1, keepdims=True)
    byte = np.maximum(np.where(amax > 0, np.frexp(amax)[1] - 1 + 127, 0) - down, 1)
    scale = np.exp2(byte - 127.0)
    codes = (blocks / scale).astype(np.float32).astype(dtype).astype(np.float64)
    return np.moveaxis((codes * scale).reshape(v.shape), -1, axis)


WIDE = False


def mx_kscale(k):
    if not WIDE:
        return np.ones(k)
    levels = np.array([10, -10, 5, -5, 0])
    if k % 512:
        return np.exp2(np.random.permutation(np.resize(levels, k // 32))).repeat(32)
    a = np.empty((k // 512, 16))
    for p in range(k // 512):
        a[p, :8] = np.random.permutation(np.resize(levels, 8))
        for g in range(8):
            far = levels[np.abs(levels - a[p, g]) >= 10]
            a[p, g + 8] = far[np.random.randint(len(far))]
    return np.exp2(a.ravel()).repeat(32)


def f64(x):
    return np.asarray(x).astype(np.float64)


def striped(idx):
    return np.tile(np.asarray(idx).reshape(-1, 16).T, (8, 1)).astype(np.uint16)


def unstriped(offs):
    return offs[:16].T.reshape(-1).astype(np.int64)


E2M1 = np.array([0.0, 0.5, 1.0, 1.5, 2.0, 3.0, 4.0, 6.0, -0.0, -0.5, -1.0, -1.5, -2.0, -3.0, -4.0, -6.0])


def pack_weight(w, fmt):
    k, n = w.shape
    w = f64(np.asarray(w, np.float32).astype(ml_dtypes.bfloat16)).reshape(k // 32, 32, n)
    amax = np.abs(w).max(1)
    if fmt == "e4m3":
        byte = np.frexp(amax)[1] - 1 + 127 - 7
    else:
        mant, ex = np.frexp(amax / 6.0)
        byte = np.where(mant > 0.5, ex, ex - 1) + 127
    byte = np.clip(np.where(amax > 0, byte, 1), 1, 254)
    scaled = (w * np.exp2(127.0 - byte)[:, None, :]).reshape(k, n).astype(np.float32)
    by_word = np.ascontiguousarray(scaled.reshape(k // 512, 128, 4, n).transpose(0, 1, 3, 2))
    if fmt == "e4m3":
        words = by_word.astype(ml_dtypes.float8_e4m3fn).view(np.uint8)
    else:
        c = by_word.astype(ml_dtypes.float4_e2m1fn).view(np.uint8) & 0xF
        words = (c[..., 0::2] | (c[..., 1::2] << 4)).reshape(k // 512, 128, 2 * n)
    return np.ascontiguousarray(words), np.ascontiguousarray(byte.astype(np.uint8).reshape(k // 512, 16, n))


def unpack_weight(words, scales, fmt):
    g, _, n = scales.shape
    words = np.ascontiguousarray(words).reshape(g, 128, n, -1)
    if fmt == "e4m3":
        vals = words.view(ml_dtypes.float8_e4m3fn).astype(np.float64)
    else:
        nib = np.empty((g, 128, n, 4), np.uint8)
        nib[..., 0::2] = words & 0xF
        nib[..., 1::2] = words >> 4
        vals = E2M1[nib]
    vals = vals * np.repeat(np.exp2(scales.astype(np.float64) - 127.0), 8, axis=1)[..., None]
    return vals.transpose(0, 1, 3, 2).reshape(g * 512, n)


D, T, I, J, Q = 1024, 4096, 1024, 512, 128


def setup_inputs():
    n = np.random.standard_normal
    idx = np.random.permutation(T)[:I]
    idx2 = np.random.randint(0, I, J)
    idx3 = np.random.randint(0, I, J)
    idx4 = np.random.randint(0, I, J)
    fd = mx_kscale(D)
    vocp = pack_weight(n((D, T)) / fd[:, None], "e2m1")
    return {
        "hid": (n((D, Q)) * 1.0 / np.sqrt(D) * fd[:, None]).astype(np.float32),
        "voc_words": vocp[0],
        "voc_scales": vocp[1],
        "lse": (np.random.uniform(7.0, 8.0, (Q, 1))).astype(np.float32),
        "offs": striped(idx),
        "offs2": striped(idx2),
        "offs3": striped(idx3),
        "offs4": striped(idx4),
    }


def reference(hid, voc_words, voc_scales, lse, offs, offs2, offs3, offs4):
    idx = unstriped(offs)
    idx2 = unstriped(offs2)
    idx3 = unstriped(offs3)
    idx4 = unstriped(offs4)
    vocu = unpack_weight(voc_words, voc_scales, "e2m1")
    hidq = mxq(f64(hid), 0, "e4m3")
    vocidxg = vocu[:, idx]
    a = hidq.T @ vocidxg
    b = a - f64(lse)
    y = b[:, idx2] + b[:, idx3] + b[:, idx4]
    return y

@@ -1,0 +1,140 @@
+from contextlib import ExitStack
+
+import concourse.mybir as mybir
+
+D, T, I, J, Q = 1024, 4096, 1024, 512, 128
+FLOPS = 2 * D * I * Q
+
+F32 = mybir.dt.float32
+BF16 = mybir.dt.bfloat16
+I32 = mybir.dt.int32
+U32 = mybir.dt.uint32
+U16 = mybir.dt.uint16
+U8 = mybir.dt.uint8
+FP8X4 = mybir.dt.float8_e4m3fn_x4
+FP4X4 = mybir.dt.float4_e2m1fn_x4
+ALU = mybir.AluOpType
+ACT = mybir.ActivationFunctionType
+
+P = 128
+PACK = 4
+K_PASS = P * PACK
+PASSES = D // K_PASS
+LIST_ROWS = 16
+HALF = I // 2
+NARROW = 128
+ROW0 = 96
+
+
+def tile_attend_treepaths_kernel(tc, hid, voc_words, voc_scales, lse, offs, offs2, offs3, offs4, out):
+    nc = tc.nc
+    with ExitStack() as ctx:
+        keep = ctx.enter_context(tc.tile_pool(name="keep", bufs=1))
+        psum = ctx.enter_context(tc.psum_pool(name="psum", bufs=1))
+
+        node_list = keep.tile([P, I // LIST_ROWS], U16, name="node_list")
+        nc.sync.dma_start(node_list[:], offs)
+
+        scale_table = keep.tile([P, T], U8, name="scale_table", align_bytes=64)
+        nc.vector.memset(scale_table[0:ROW0, :].bitcast(I32), 0)
+        nc.sync.dma_start(
+            scale_table[ROW0:P, :].bitcast(I32),
+            voc_scales.bitcast(I32).rearrange("z f c -> f z c"),
+        )
+
+        lse_col = keep.tile([P, 1], F32, name="lse_col")
+        nc.sync.dma_start(lse_col[:], lse)
+        step_lists = []
+        for s, src in enumerate((offs2, offs3, offs4)):
+            step_list = keep.tile([P, J // LIST_ROWS], U16, name="step_list%d" % s)
+            nc.sync.dma_start(step_list[:], src)
+            step_lists.append(step_list)
+
+        word_tables, hid_rows = [], []
+        for z in range(PASSES):
+            word_table = keep.tile([P, T], U16, name="word_table%d" % z, align_bytes=64)
+            nc.sync.dma_start(word_table[:].bitcast(I32), voc_words[z].bitcast(I32))
+            word_tables.append(word_table)
+            rows = keep.tile([P, PACK, Q], F32, name="hid_rows%d" % z, align_bytes=64)
+            nc.sync.dma_start(
+                rows[:], hid[z * K_PASS : (z + 1) * K_PASS, :].rearrange("(p t) q -> p t q", t=PACK)
+            )
+            hid_rows.append(rows)
+
+        node_planes = keep.tile([P, PASSES * I], U8, name="node_planes", align_bytes=64)
+        nc.vector.memset(node_planes[:].bitcast(I32), 0)
+
+        neg_lse = keep.tile([P, 1], F32, name="neg_lse")
+        nc.scalar.activation(neg_lse[:], lse_col[:], ACT.Identity, scale=-1.0)
+
+        node_scales = keep.tile([P, I], U8, name="node_scales", align_bytes=64)
+        nc.vector.tensor_copy(node_scales[:], scale_table[:].indirect(node_list[:]))
+        for quad in range(4):
+            first = ROW0 + 8 * quad
+            nc.scalar.dma_start(
+                node_planes[32 * quad : 32 * quad + 4, :].bitcast(I32),
+                node_scales[first : first + 8, :].bitcast(I32),
+            )
+
+        chunks = [(0, HALF)] + [(c, NARROW) for c in range(HALF, I, NARROW)]
+        banks = [psum.tile([Q, width], F32, name="bank%d" % c) for c, (start, width) in enumerate(chunks)]
+        logp = keep.tile([Q, I], F32, name="logp", align_bytes=64)
+
+        for z in range(PASSES):
+            grouped = keep.tile([P, Q, PACK], BF16, name="grouped%d" % z, align_bytes=64)
+            nc.scalar.copy(
+                grouped[:].rearrange("p (c i) t -> p c t i", i=4),
+                hid_rows[z][:].rearrange("p t (c i) -> p c t i", i=4),
+            )
+            hid_codes = keep.tile([P, Q], U32, name="hid_codes%d" % z, align_bytes=64)
+            hid_plane = keep.tile([P, Q], U8, name="hid_plane%d" % z, align_bytes=64)
+            pieces = [(0, I)] if z == 0 else [(0, HALF), (HALF, HALF)]
+            node_words = []
+            for n, (start, width) in enumerate(pieces):
+                words = keep.tile([P, width], U16, name="node_words%d_%d" % (z, n), align_bytes=64)
+                nc.vector.tensor_copy(
+                    words[:],
+                    word_tables[z][:].indirect(node_list[:, start // LIST_ROWS : (start + width) // LIST_ROWS]),
+                )
+                node_words.append(words)
+                if n == 0:
+                    nc.vector.quantize_mx(
+                        out=hid_codes[:].bitcast(FP8X4),
+                        scales=hid_plane[:],
+                        in_=grouped[:].rearrange("p q t -> p (q t)"),
+                    )
+            for c, (start, width) in enumerate(chunks):
+                n = 0 if z == 0 else start // HALF
+                local = start - pieces[n][0]
+                nc.tensor.matmul_mx(
+                    out=banks[c][:],
+                    lhsT=hid_codes[:].bitcast(FP8X4),
+                    lhsT_scale=hid_plane[:],
+                    rhs=node_words[n][:, local : local + width].bitcast(FP4X4),
+                    rhs_scale=node_planes[:, z * I + start : z * I + start + width],
+                    start=(z == 0),
+                    stop=(z == PASSES - 1),
+                )
+
+        for c, (start, width) in enumerate(chunks):
+            if c % 2 == 0:
+                nc.scalar.activation(logp[:, start : start + width], banks[c][:], ACT.Identity, bias=neg_lse[:])
+            else:
+                nc.vector.tensor_scalar(logp[:, start : start + width], banks[c][:], lse_col[:], None, ALU.subtract)
+
+        parts = 2
+        width = J // parts
+        sums = [None] * parts
+        for s, step_list in enumerate(step_lists):
+            for h in range(parts):
+                looked_up = logp[:].indirect(
+                    step_list[:, h * width // LIST_ROWS : (h + 1) * width // LIST_ROWS]
+                )
+                total = keep.tile([Q, width], F32, name="sum%d_%d" % (s, h), align_bytes=64)
+                if s == 0:
+                    nc.vector.tensor_copy(total[:], looked_up)
+                else:
+                    nc.vector.tensor_tensor(total[:], looked_up, sums[h][:], ALU.add)
+                sums[h] = total
+        for h in range(parts):
+            nc.sync.dma_start(out[:, h * width : (h + 1) * width], sums[h][:])

@@ -32,34 +32,33 @@ def tile_attend_treepaths_kernel(tc, hid, voc_words, voc_scales, lse, offs, offs
         keep = ctx.enter_context(tc.tile_pool(name="keep", bufs=1))
         psum = ctx.enter_context(tc.psum_pool(name="psum", bufs=1))
 
-        node_list = keep.tile([P, I // LIST_ROWS], U16, name="node_list")
-        nc.sync.dma_start(node_list[:], offs)
-
         scale_table = keep.tile([P, T], U8, name="scale_table", align_bytes=64)
         nc.vector.memset(scale_table[0:ROW0, :].bitcast(I32), 0)
         nc.sync.dma_start(
             scale_table[ROW0:P, :].bitcast(I32),
             voc_scales.bitcast(I32).rearrange("z f c -> f z c"),
         )
+        node_list = keep.tile([P, I // LIST_ROWS], U16, name="node_list")
+        nc.sync.dma_start(node_list[:], offs)
 
         lse_col = keep.tile([P, 1], F32, name="lse_col")
-        nc.sync.dma_start(lse_col[:], lse)
-        step_lists = []
-        for s, src in enumerate((offs2, offs3, offs4)):
-            step_list = keep.tile([P, J // LIST_ROWS], U16, name="step_list%d" % s)
-            nc.sync.dma_start(step_list[:], src)
-            step_lists.append(step_list)
+        nc.scalar.dma_start(lse_col[:], lse)
+        step_lists = [keep.tile([P, J // LIST_ROWS], U16, name="step_list%d" % s) for s in range(3)]
 
         word_tables, hid_rows = [], []
         for z in range(PASSES):
             word_table = keep.tile([P, T], U16, name="word_table%d" % z, align_bytes=64)
             nc.sync.dma_start(word_table[:].bitcast(I32), voc_words[z].bitcast(I32))
             word_tables.append(word_table)
+            if z == 0:
+                nc.sync.dma_start(step_lists[0][:], offs2)
+                nc.sync.dma_start(step_lists[1][:], offs3)
             rows = keep.tile([P, PACK, Q], F32, name="hid_rows%d" % z, align_bytes=64)
             nc.sync.dma_start(
                 rows[:], hid[z * K_PASS : (z + 1) * K_PASS, :].rearrange("(p t) q -> p t q", t=PACK)
             )
             hid_rows.append(rows)
+        nc.sync.dma_start(step_lists[2][:], offs4)
 
         node_planes = keep.tile([P, PASSES * I], U8, name="node_planes", align_bytes=64)
         nc.vector.memset(node_planes[:].bitcast(I32), 0)
@@ -81,7 +80,7 @@ def tile_attend_treepaths_kernel(tc, hid, voc_words, voc_scales, lse, offs, offs
         logp = keep.tile([Q, I], F32, name="logp", align_bytes=64)
 
         for z in range(PASSES):
-            grouped = keep.tile([P, Q, PACK], BF16, name="grouped%d" % z, align_bytes=64)
+            grouped = keep.tile([P, Q, PACK], BF16, name="grouped%d" % z, tag="held%d" % z, align_bytes=64)
             nc.scalar.copy(
                 grouped[:].rearrange("p (c i) t -> p c t i", i=4),
                 hid_rows[z][:].rearrange("p t (c i) -> p c t i", i=4),
@@ -91,7 +90,8 @@ def tile_attend_treepaths_kernel(tc, hid, voc_words, voc_scales, lse, offs, offs
             pieces = [(0, I)] if z == 0 else [(0, HALF), (HALF, HALF)]
             node_words = []
             for n, (start, width) in enumerate(pieces):
-                words = keep.tile([P, width], U16, name="node_words%d_%d" % (z, n), align_bytes=64)
+                tag = "held1" if n == 1 else "words%d" % z
+                words = keep.tile([P, width], U16, name="node_words%d_%d" % (z, n), tag=tag, align_bytes=64)
                 nc.vector.tensor_copy(
                     words[:],
                     word_tables[z][:].indirect(node_list[:, start // LIST_ROWS : (start + width) // LIST_ROWS]),
@@ -122,19 +122,16 @@ def tile_attend_treepaths_kernel(tc, hid, voc_words, voc_scales, lse, offs, offs
             else:
                 nc.vector.tensor_scalar(logp[:, start : start + width], banks[c][:], lse_col[:], None, ALU.subtract)
 
-        parts = 2
-        width = J // parts
-        sums = [None] * parts
+        parts = [(0, 320), (320, 192)]
+        sums = [None] * len(parts)
         for s, step_list in enumerate(step_lists):
-            for h in range(parts):
-                looked_up = logp[:].indirect(
-                    step_list[:, h * width // LIST_ROWS : (h + 1) * width // LIST_ROWS]
-                )
+            for h, (start, width) in enumerate(parts):
+                looked_up = logp[:].indirect(step_list[:, start // LIST_ROWS : (start + width) // LIST_ROWS])
                 total = keep.tile([Q, width], F32, name="sum%d_%d" % (s, h), align_bytes=64)
                 if s == 0:
                     nc.vector.tensor_copy(total[:], looked_up)
                 else:
                     nc.vector.tensor_tensor(total[:], looked_up, sums[h][:], ALU.add)
                 sums[h] = total
-        for h in range(parts):
-            nc.sync.dma_start(out[:, h * width : (h + 1) * width], sums[h][:])
+        for h, (start, width) in enumerate(parts):
+            nc.sync.dma_start(out[:, start : start + width], sums[h][:])

@@ -42,7 +42,7 @@ def tile_attend_treepaths_kernel(tc, hid, voc_words, voc_scales, lse, offs, offs
         nc.sync.dma_start(node_list[:], offs)
 
         lse_col = keep.tile([P, 1], F32, name="lse_col")
-        nc.scalar.dma_start(lse_col[:], lse)
+        nc.sync.dma_start(lse_col[:], lse)
         step_lists = [keep.tile([P, J // LIST_ROWS], U16, name="step_list%d" % s) for s in range(3)]
 
         word_tables, hid_rows = [], []

@@ -70,7 +70,7 @@ def tile_attend_treepaths_kernel(tc, hid, voc_words, voc_scales, lse, offs, offs
         nc.vector.tensor_copy(node_scales[:], scale_table[:].indirect(node_list[:]))
         for quad in range(4):
             first = ROW0 + 8 * quad
-            nc.scalar.dma_start(
+            nc.sync.dma_start(
                 node_planes[32 * quad : 32 * quad + 4, :].bitcast(I32),
                 node_scales[first : first + 8, :].bitcast(I32),
             )

@@ -53,7 +53,7 @@ def tile_attend_treepaths_kernel(tc, hid, voc_words, voc_scales, lse, offs, offs
             if z == 0:
                 nc.sync.dma_start(step_lists[0][:], offs2)
                 nc.sync.dma_start(step_lists[1][:], offs3)
-            rows = keep.tile([P, PACK, Q], F32, name="hid_rows%d" % z, align_bytes=64)
+            rows = keep.tile([P, PACK, Q], F32, name="hid_rows%d" % z, tag="held%d" % z, align_bytes=64)
             nc.sync.dma_start(
                 rows[:], hid[z * K_PASS : (z + 1) * K_PASS, :].rearrange("(p t) q -> p t q", t=PACK)
             )
@@ -80,7 +80,7 @@ def tile_attend_treepaths_kernel(tc, hid, voc_words, voc_scales, lse, offs, offs
         logp = keep.tile([Q, I], F32, name="logp", align_bytes=64)
 
         for z in range(PASSES):
-            grouped = keep.tile([P, Q, PACK], BF16, name="grouped%d" % z, tag="held%d" % z, align_bytes=64)
+            grouped = keep.tile([P, Q, PACK], BF16, name="grouped%d" % z, align_bytes=64)
             nc.scalar.copy(
                 grouped[:].rearrange("p (c i) t -> p c t i", i=4),
                 hid_rows[z][:].rearrange("p t (c i) -> p c t i", i=4),

@@ -42,7 +42,6 @@ def tile_attend_treepaths_kernel(tc, hid, voc_words, voc_scales, lse, offs, offs
         nc.sync.dma_start(node_list[:], offs)
 
         lse_col = keep.tile([P, 1], F32, name="lse_col")
-        nc.sync.dma_start(lse_col[:], lse)
         step_lists = [keep.tile([P, J // LIST_ROWS], U16, name="step_list%d" % s) for s in range(3)]
 
         word_tables, hid_rows = [], []
@@ -58,17 +57,15 @@ def tile_attend_treepaths_kernel(tc, hid, voc_words, voc_scales, lse, offs, offs
                 rows[:], hid[z * K_PASS : (z + 1) * K_PASS, :].rearrange("(p t) q -> p t q", t=PACK)
             )
             hid_rows.append(rows)
+        nc.sync.dma_start(lse_col[:], lse)
         nc.sync.dma_start(step_lists[2][:], offs4)
 
         node_planes = keep.tile([P, PASSES * I], U8, name="node_planes", align_bytes=64)
         nc.vector.memset(node_planes[:].bitcast(I32), 0)
 
-        neg_lse = keep.tile([P, 1], F32, name="neg_lse")
-        nc.scalar.activation(neg_lse[:], lse_col[:], ACT.Identity, scale=-1.0)
-
         node_scales = keep.tile([P, I], U8, name="node_scales", align_bytes=64)
         nc.vector.tensor_copy(node_scales[:], scale_table[:].indirect(node_list[:]))
-        for quad in range(4):
+        for quad in (0, 2, 1, 3):
             first = ROW0 + 8 * quad
             nc.sync.dma_start(
                 node_planes[32 * quad : 32 * quad + 4, :].bitcast(I32),
@@ -79,6 +76,7 @@ def tile_attend_treepaths_kernel(tc, hid, voc_words, voc_scales, lse, offs, offs
         banks = [psum.tile([Q, width], F32, name="bank%d" % c) for c, (start, width) in enumerate(chunks)]
         logp = keep.tile([Q, I], F32, name="logp", align_bytes=64)
 
+        operands = []
         for z in range(PASSES):
             grouped = keep.tile([P, Q, PACK], BF16, name="grouped%d" % z, align_bytes=64)
             nc.scalar.copy(
@@ -103,26 +101,38 @@ def tile_attend_treepaths_kernel(tc, hid, voc_words, voc_scales, lse, offs, offs
                         scales=hid_plane[:],
                         in_=grouped[:].rearrange("p q t -> p (q t)"),
                     )
-            for c, (start, width) in enumerate(chunks):
-                n = 0 if z == 0 else start // HALF
-                local = start - pieces[n][0]
-                nc.tensor.matmul_mx(
-                    out=banks[c][:],
-                    lhsT=hid_codes[:].bitcast(FP8X4),
-                    lhsT_scale=hid_plane[:],
-                    rhs=node_words[n][:, local : local + width].bitcast(FP4X4),
-                    rhs_scale=node_planes[:, z * I + start : z * I + start + width],
-                    start=(z == 0),
-                    stop=(z == PASSES - 1),
-                )
+            operands.append((hid_codes, hid_plane, pieces, node_words))
 
+        def multiply(z, c):
+            hid_codes, hid_plane, pieces, node_words = operands[z]
+            start, width = chunks[c]
+            n = 0 if z == 0 else start // HALF
+            local = start - pieces[n][0]
+            nc.tensor.matmul_mx(
+                out=banks[c][:],
+                lhsT=hid_codes[:].bitcast(FP8X4),
+                lhsT_scale=hid_plane[:],
+                rhs=node_words[n][:, local : local + width].bitcast(FP4X4),
+                rhs_scale=node_planes[:, z * I + start : z * I + start + width],
+                start=(z == 0),
+                stop=(z == PASSES - 1),
+            )
+
+        for z in range(PASSES):
+            multiply(z, 0)
+        for z in range(PASSES):
+            for c in range(1, len(chunks)):
+                multiply(z, c)
+
+        neg_lse = keep.tile([P, 1], F32, name="neg_lse")
+        nc.scalar.activation(neg_lse[:], lse_col[:], ACT.Identity, scale=-1.0)
         for c, (start, width) in enumerate(chunks):
             if c % 2 == 0:
                 nc.scalar.activation(logp[:, start : start + width], banks[c][:], ACT.Identity, bias=neg_lse[:])
             else:
                 nc.vector.tensor_scalar(logp[:, start : start + width], banks[c][:], lse_col[:], None, ALU.subtract)
 
-        parts = [(0, 320), (320, 192)]
+        parts = [(0, 352), (352, 160)]
         sums = [None] * len(parts)
         for s, step_list in enumerate(step_lists):
             for h, (start, width) in enumerate(parts):

@@ -32,6 +32,8 @@ def tile_attend_treepaths_kernel(tc, hid, voc_words, voc_scales, lse, offs, offs
         keep = ctx.enter_context(tc.tile_pool(name="keep", bufs=1))
         psum = ctx.enter_context(tc.psum_pool(name="psum", bufs=1))
 
+        lse_rows = keep.tile([P, 32], F32, name="lse_rows", align_bytes=64)
+        nc.vector.memset(lse_rows[:], 0.0)
         scale_table = keep.tile([P, T], U8, name="scale_table", align_bytes=64)
         nc.vector.memset(scale_table[0:ROW0, :].bitcast(I32), 0)
         nc.sync.dma_start(
@@ -41,7 +43,6 @@ def tile_attend_treepaths_kernel(tc, hid, voc_words, voc_scales, lse, offs, offs
         node_list = keep.tile([P, I // LIST_ROWS], U16, name="node_list")
         nc.sync.dma_start(node_list[:], offs)
 
-        lse_col = keep.tile([P, 1], F32, name="lse_col")
         step_lists = [keep.tile([P, J // LIST_ROWS], U16, name="step_list%d" % s) for s in range(3)]
 
         word_tables, hid_rows = [], []
@@ -50,14 +51,14 @@ def tile_attend_treepaths_kernel(tc, hid, voc_words, voc_scales, lse, offs, offs
             nc.sync.dma_start(word_table[:].bitcast(I32), voc_words[z].bitcast(I32))
             word_tables.append(word_table)
             if z == 0:
+                nc.sync.dma_start(lse_rows[0:P:32, :], lse.rearrange("(g i) o -> g (i o)", i=32))
                 nc.sync.dma_start(step_lists[0][:], offs2)
-                nc.sync.dma_start(step_lists[1][:], offs3)
             rows = keep.tile([P, PACK, Q], F32, name="hid_rows%d" % z, tag="held%d" % z, align_bytes=64)
             nc.sync.dma_start(
                 rows[:], hid[z * K_PASS : (z + 1) * K_PASS, :].rearrange("(p t) q -> p t q", t=PACK)
             )
             hid_rows.append(rows)
-        nc.sync.dma_start(lse_col[:], lse)
+        nc.sync.dma_start(step_lists[1][:], offs3)
         nc.sync.dma_start(step_lists[2][:], offs4)
 
         node_planes = keep.tile([P, PASSES * I], U8, name="node_planes", align_bytes=64)
@@ -78,7 +79,7 @@ def tile_attend_treepaths_kernel(tc, hid, voc_words, voc_scales, lse, offs, offs
 
         operands = []
         for z in range(PASSES):
-            grouped = keep.tile([P, Q, PACK], BF16, name="grouped%d" % z, align_bytes=64)
+            grouped = keep.tile([P, Q, PACK], BF16, name="grouped%d" % z, tag="grouped%d" % z, align_bytes=64)
             nc.scalar.copy(
                 grouped[:].rearrange("p (c i) t -> p c t i", i=4),
                 hid_rows[z][:].rearrange("p t (c i) -> p c t i", i=4),
@@ -124,13 +125,16 @@ def tile_attend_treepaths_kernel(tc, hid, voc_words, voc_scales, lse, offs, offs
             for c in range(1, len(chunks)):
                 multiply(z, c)
 
-        neg_lse = keep.tile([P, 1], F32, name="neg_lse")
-        nc.scalar.activation(neg_lse[:], lse_col[:], ACT.Identity, scale=-1.0)
+        lse_turned = keep.tile([P, 32], F32, name="lse_turned", align_bytes=64)
+        nc.vector.transpose(lse_turned[:], lse_rows[:])
+        lse_col = lse_turned[:, 0:1]
+        neg_lse = keep.tile([P, 1], F32, name="neg_lse", tag="grouped1", align_bytes=64)
+        nc.scalar.activation(neg_lse[:], lse_col, ACT.Identity, scale=-1.0)
         for c, (start, width) in enumerate(chunks):
             if c % 2 == 0:
                 nc.scalar.activation(logp[:, start : start + width], banks[c][:], ACT.Identity, bias=neg_lse[:])
             else:
-                nc.vector.tensor_scalar(logp[:, start : start + width], banks[c][:], lse_col[:], None, ALU.subtract)
+                nc.vector.tensor_scalar(logp[:, start : start + width], banks[c][:], lse_col, None, ALU.subtract)
 
         parts = [(0, 352), (352, 160)]
         sums = [None] * len(parts)

@@ -136,7 +136,7 @@ def tile_attend_treepaths_kernel(tc, hid, voc_words, voc_scales, lse, offs, offs
             else:
                 nc.vector.tensor_scalar(logp[:, start : start + width], banks[c][:], lse_col, None, ALU.subtract)
 
-        parts = [(0, 352), (352, 160)]
+        parts = [(0, 256), (256, 256)]
         sums = [None] * len(parts)
         for s, step_list in enumerate(step_lists):
             for h, (start, width) in enumerate(parts):

@@ -136,16 +136,23 @@ def tile_attend_treepaths_kernel(tc, hid, voc_words, voc_scales, lse, offs, offs
             else:
                 nc.vector.tensor_scalar(logp[:, start : start + width], banks[c][:], lse_col, None, ALU.subtract)
 
-        parts = [(0, 256), (256, 256)]
-        sums = [None] * len(parts)
-        for s, step_list in enumerate(step_lists):
-            for h, (start, width) in enumerate(parts):
-                looked_up = logp[:].indirect(step_list[:, start // LIST_ROWS : (start + width) // LIST_ROWS])
-                total = keep.tile([Q, width], F32, name="sum%d_%d" % (s, h), align_bytes=64)
-                if s == 0:
-                    nc.vector.tensor_copy(total[:], looked_up)
-                else:
-                    nc.vector.tensor_tensor(total[:], looked_up, sums[h][:], ALU.add)
-                sums[h] = total
-        for h, (start, width) in enumerate(parts):
-            nc.sync.dma_start(out[:, start : start + width], sums[h][:])
+        def listed(s, start, width):
+            return logp[:].indirect(step_lists[s][:, start // LIST_ROWS : (start + width) // LIST_ROWS])
+
+        def fresh(name, width):
+            return keep.tile([Q, width], F32, name=name, align_bytes=64)
+
+        W = J // 2
+        y1, y2, y3 = fresh("y1", W), fresh("y2", W), fresh("y3", W)
+        x1, x2, x3 = fresh("x1", W), fresh("x2", W), fresh("x3", W)
+        out_a, out_b = fresh("out_a", W), fresh("out_b", W)
+        nc.scalar.activation(y1[:], listed(0, 0, W), ACT.Copy)
+        nc.scalar.activation(y2[:], listed(0, W, W), ACT.Copy)
+        nc.scalar.activation(y3[:], listed(1, W, W), ACT.Copy)
+        nc.vector.tensor_copy(x1[:], listed(2, W, W))
+        nc.vector.tensor_tensor(x2[:], listed(2, 0, W), y1[:], ALU.add)
+        nc.vector.tensor_tensor(x3[:], x1[:], y2[:], ALU.add)
+        nc.vector.tensor_tensor(out_a[:], listed(1, 0, W), x2[:], ALU.add)
+        nc.vector.tensor_tensor(out_b[:], x3[:], y3[:], ALU.add)
+        nc.sync.dma_start(out[:, 0:W], out_a[:])
+        nc.sync.dma_start(out[:, W:J], out_b[:])

@@ -143,16 +143,19 @@ def tile_attend_treepaths_kernel(tc, hid, voc_words, voc_scales, lse, offs, offs
             return keep.tile([Q, width], F32, name=name, align_bytes=64)
 
         W = J // 2
+        N = W // 2
         y1, y2, y3 = fresh("y1", W), fresh("y2", W), fresh("y3", W)
-        x1, x2, x3 = fresh("x1", W), fresh("x2", W), fresh("x3", W)
+        x1a, x1b, x2, x3 = fresh("x1a", N), fresh("x1b", N), fresh("x2", W), fresh("x3", W)
         out_a, out_b = fresh("out_a", W), fresh("out_b", W)
-        nc.scalar.activation(y1[:], listed(0, 0, W), ACT.Copy)
-        nc.scalar.activation(y2[:], listed(0, W, W), ACT.Copy)
+        nc.scalar.activation(y1[:], listed(0, W, W), ACT.Copy)
+        nc.scalar.activation(y2[:], listed(0, 0, W), ACT.Copy)
         nc.scalar.activation(y3[:], listed(1, W, W), ACT.Copy)
-        nc.vector.tensor_copy(x1[:], listed(2, W, W))
-        nc.vector.tensor_tensor(x2[:], listed(2, 0, W), y1[:], ALU.add)
-        nc.vector.tensor_tensor(x3[:], x1[:], y2[:], ALU.add)
-        nc.vector.tensor_tensor(out_a[:], listed(1, 0, W), x2[:], ALU.add)
+        nc.vector.tensor_copy(x1a[:], listed(2, 0, N))
+        nc.vector.tensor_copy(x1b[:], listed(2, N, N))
+        nc.vector.tensor_tensor(x2[:, 0:N], listed(1, 0, N), x1a[:], ALU.add)
+        nc.vector.tensor_tensor(x2[:, N:W], listed(1, N, N), x1b[:], ALU.add)
+        nc.vector.tensor_tensor(x3[:], listed(2, W, W), y1[:], ALU.add)
+        nc.vector.tensor_tensor(out_a[:], x2[:], y2[:], ALU.add)
         nc.vector.tensor_tensor(out_b[:], x3[:], y3[:], ALU.add)
         nc.sync.dma_start(out[:, 0:W], out_a[:])
         nc.sync.dma_start(out[:, W:J], out_b[:])

@@ -149,13 +149,15 @@ def tile_attend_treepaths_kernel(tc, hid, voc_words, voc_scales, lse, offs, offs
         out_a, out_b = fresh("out_a", W), fresh("out_b", W)
         nc.scalar.activation(y1[:], listed(0, W, W), ACT.Copy)
         nc.scalar.activation(y2[:], listed(0, 0, W), ACT.Copy)
-        nc.scalar.activation(y3[:], listed(1, W, W), ACT.Copy)
+        nc.scalar.activation(y3[:, 0:N], listed(1, W, N), ACT.Copy)
+        nc.scalar.activation(y3[:, N:W], listed(1, W + N, N), ACT.Copy)
         nc.vector.tensor_copy(x1a[:], listed(2, 0, N))
         nc.vector.tensor_copy(x1b[:], listed(2, N, N))
         nc.vector.tensor_tensor(x2[:, 0:N], listed(1, 0, N), x1a[:], ALU.add)
         nc.vector.tensor_tensor(x2[:, N:W], listed(1, N, N), x1b[:], ALU.add)
         nc.vector.tensor_tensor(x3[:], listed(2, W, W), y1[:], ALU.add)
         nc.vector.tensor_tensor(out_a[:], x2[:], y2[:], ALU.add)
-        nc.vector.tensor_tensor(out_b[:], x3[:], y3[:], ALU.add)
+        nc.vector.tensor_tensor(out_b[:, 0:N], x3[:, 0:N], y3[:, 0:N], ALU.add)
+        nc.vector.tensor_tensor(out_b[:, N:W], x3[:, N:W], y3[:, N:W], ALU.add)
         nc.sync.dma_start(out[:, 0:W], out_a[:])
         nc.sync.dma_start(out[:, W:J], out_b[:])

@@ -34,6 +34,7 @@ def tile_attend_treepaths_kernel(tc, hid, voc_words, voc_scales, lse, offs, offs
 
         lse_rows = keep.tile([P, 32], F32, name="lse_rows", align_bytes=64)
         nc.vector.memset(lse_rows[:], 0.0)
+        nc.scalar.dma_start(lse_rows[0:P:32, :], lse.rearrange("(g i) o -> g (i o)", i=32))
         scale_table = keep.tile([P, T], U8, name="scale_table", align_bytes=64)
         nc.vector.memset(scale_table[0:ROW0, :].bitcast(I32), 0)
         nc.sync.dma_start(
@@ -51,7 +52,6 @@ def tile_attend_treepaths_kernel(tc, hid, voc_words, voc_scales, lse, offs, offs
             nc.sync.dma_start(word_table[:].bitcast(I32), voc_words[z].bitcast(I32))
             word_tables.append(word_table)
             if z == 0:
-                nc.sync.dma_start(lse_rows[0:P:32, :], lse.rearrange("(g i) o -> g (i o)", i=32))
                 nc.sync.dma_start(step_lists[0][:], offs2)
             rows = keep.tile([P, PACK, Q], F32, name="hid_rows%d" % z, tag="held%d" % z, align_bytes=64)
             nc.sync.dma_start(
@@ -63,6 +63,9 @@ def tile_attend_treepaths_kernel(tc, hid, voc_words, voc_scales, lse, offs, offs
 
         node_planes = keep.tile([P, PASSES * I], U8, name="node_planes", align_bytes=64)
         nc.vector.memset(node_planes[:].bitcast(I32), 0)
+
+        lse_turned = keep.tile([P, 32], F32, name="lse_turned", align_bytes=64)
+        nc.vector.transpose(lse_turned[:], lse_rows[:])
 
         node_scales = keep.tile([P, I], U8, name="node_scales", align_bytes=64)
         nc.vector.tensor_copy(node_scales[:], scale_table[:].indirect(node_list[:]))
@@ -80,10 +83,12 @@ def tile_attend_treepaths_kernel(tc, hid, voc_words, voc_scales, lse, offs, offs
         operands = []
         for z in range(PASSES):
             grouped = keep.tile([P, Q, PACK], BF16, name="grouped%d" % z, tag="grouped%d" % z, align_bytes=64)
-            nc.scalar.copy(
-                grouped[:].rearrange("p (c i) t -> p c t i", i=4),
-                hid_rows[z][:].rearrange("p t (c i) -> p c t i", i=4),
-            )
+            spans = [(0, Q)] if z == 0 else [(0, Q // 2), (Q // 2, Q)]
+            for lo, hi in spans:
+                nc.scalar.copy(
+                    grouped[:, lo:hi, :].rearrange("p (c i) t -> p c t i", i=4),
+                    hid_rows[z][:, :, lo:hi].rearrange("p t (c i) -> p c t i", i=4),
+                )
             hid_codes = keep.tile([P, Q], U32, name="hid_codes%d" % z, align_bytes=64)
             hid_plane = keep.tile([P, Q], U8, name="hid_plane%d" % z, align_bytes=64)
             pieces = [(0, I)] if z == 0 else [(0, HALF), (HALF, HALF)]
@@ -97,11 +102,12 @@ def tile_attend_treepaths_kernel(tc, hid, voc_words, voc_scales, lse, offs, offs
                 )
                 node_words.append(words)
                 if n == 0:
-                    nc.vector.quantize_mx(
-                        out=hid_codes[:].bitcast(FP8X4),
-                        scales=hid_plane[:],
-                        in_=grouped[:].rearrange("p q t -> p (q t)"),
-                    )
+                    for lo, hi in spans:
+                        nc.vector.quantize_mx(
+                            out=hid_codes[:, lo:hi].bitcast(FP8X4),
+                            scales=hid_plane[:, lo:hi],
+                            in_=grouped[:, lo:hi, :].rearrange("p q t -> p (q t)"),
+                        )
             operands.append((hid_codes, hid_plane, pieces, node_words))
 
         def multiply(z, c):
@@ -125,8 +131,6 @@ def tile_attend_treepaths_kernel(tc, hid, voc_words, voc_scales, lse, offs, offs
             for c in range(1, len(chunks)):
                 multiply(z, c)
 
-        lse_turned = keep.tile([P, 32], F32, name="lse_turned", align_bytes=64)
-        nc.vector.transpose(lse_turned[:], lse_rows[:])
         lse_col = lse_turned[:, 0:1]
         neg_lse = keep.tile([P, 1], F32, name="neg_lse", tag="grouped1", align_bytes=64)
         nc.scalar.activation(neg_lse[:], lse_col, ACT.Identity, scale=-1.0)

@@ -64,9 +64,6 @@ def tile_attend_treepaths_kernel(tc, hid, voc_words, voc_scales, lse, offs, offs
         node_planes = keep.tile([P, PASSES * I], U8, name="node_planes", align_bytes=64)
         nc.vector.memset(node_planes[:].bitcast(I32), 0)
 
-        lse_turned = keep.tile([P, 32], F32, name="lse_turned", align_bytes=64)
-        nc.vector.transpose(lse_turned[:], lse_rows[:])
-
         node_scales = keep.tile([P, I], U8, name="node_scales", align_bytes=64)
         nc.vector.tensor_copy(node_scales[:], scale_table[:].indirect(node_list[:]))
         for quad in (0, 2, 1, 3):
@@ -131,6 +128,8 @@ def tile_attend_treepaths_kernel(tc, hid, voc_words, voc_scales, lse, offs, offs
             for c in range(1, len(chunks)):
                 multiply(z, c)
 
+        lse_turned = keep.tile([P, 32], F32, name="lse_turned", tag="held0", align_bytes=64)
+        nc.vector.transpose(lse_turned[:], lse_rows[:])
         lse_col = lse_turned[:, 0:1]
         neg_lse = keep.tile([P, 1], F32, name="neg_lse", tag="grouped1", align_bytes=64)
         nc.scalar.activation(neg_lse[:], lse_col, ACT.Identity, scale=-1.0)

from contextlib import ExitStack

import concourse.mybir as mybir

D, T, I, J, Q = 1024, 4096, 1024, 512, 128
FLOPS = 2 * D * I * Q

F32 = mybir.dt.float32
BF16 = mybir.dt.bfloat16
I32 = mybir.dt.int32
U32 = mybir.dt.uint32
U16 = mybir.dt.uint16
U8 = mybir.dt.uint8
FP8X4 = mybir.dt.float8_e4m3fn_x4
FP4X4 = mybir.dt.float4_e2m1fn_x4
ALU = mybir.AluOpType
ACT = mybir.ActivationFunctionType

P = 128
PACK = 4
K_PASS = P * PACK
PASSES = D // K_PASS
LIST_ROWS = 16
HALF = I // 2
NARROW = 128
ROW0 = 96


def tile_attend_treepaths_kernel(tc, hid, voc_words, voc_scales, lse, offs, offs2, offs3, offs4, out):
    nc = tc.nc
    with ExitStack() as ctx:
        keep = ctx.enter_context(tc.tile_pool(name="keep", bufs=1))
        psum = ctx.enter_context(tc.psum_pool(name="psum", bufs=1))

        lse_rows = keep.tile([P, 32], F32, name="lse_rows", align_bytes=64)
        nc.vector.memset(lse_rows[:], 0.0)
        nc.scalar.dma_start(lse_rows[0:P:32, :], lse.rearrange("(g i) o -> g (i o)", i=32))
        scale_table = keep.tile([P, T], U8, name="scale_table", align_bytes=64)
        nc.vector.memset(scale_table[0:ROW0, :].bitcast(I32), 0)
        nc.sync.dma_start(
            scale_table[ROW0:P, :].bitcast(I32),
            voc_scales.bitcast(I32).rearrange("z f c -> f z c"),
        )
        node_list = keep.tile([P, I // LIST_ROWS], U16, name="node_list")
        nc.sync.dma_start(node_list[:], offs)

        step_lists = [keep.tile([P, J // LIST_ROWS], U16, name="step_list%d" % s) for s in range(3)]

        word_tables, hid_rows = [], []
        for z in range(PASSES):
            word_table = keep.tile([P, T], U16, name="word_table%d" % z, align_bytes=64)
            nc.sync.dma_start(word_table[:].bitcast(I32), voc_words[z].bitcast(I32))
            word_tables.append(word_table)
            if z == 0:
                nc.sync.dma_start(step_lists[0][:], offs2)
            rows = keep.tile([P, PACK, Q], F32, name="hid_rows%d" % z, tag="held%d" % z, align_bytes=64)
            nc.sync.dma_start(
                rows[:], hid[z * K_PASS : (z + 1) * K_PASS, :].rearrange("(p t) q -> p t q", t=PACK)
            )
            hid_rows.append(rows)
        nc.sync.dma_start(step_lists[1][:], offs3)
        nc.sync.dma_start(step_lists[2][:], offs4)

        node_planes = keep.tile([P, PASSES * I], U8, name="node_planes", align_bytes=64)
        nc.vector.memset(node_planes[:].bitcast(I32), 0)

        node_scales = keep.tile([P, I], U8, name="node_scales", align_bytes=64)
        nc.vector.tensor_copy(node_scales[:], scale_table[:].indirect(node_list[:]))
        for quad in (0, 2, 1, 3):
            first = ROW0 + 8 * quad
            nc.sync.dma_start(
                node_planes[32 * quad : 32 * quad + 4, :].bitcast(I32),
                node_scales[first : first + 8, :].bitcast(I32),
            )

        chunks = [(0, HALF)] + [(c, NARROW) for c in range(HALF, I, NARROW)]
        banks = [psum.tile([Q, width], F32, name="bank%d" % c) for c, (start, width) in enumerate(chunks)]
        logp = keep.tile([Q, I], F32, name="logp", align_bytes=64)

        operands = []
        for z in range(PASSES):
            grouped = keep.tile([P, Q, PACK], BF16, name="grouped%d" % z, tag="grouped%d" % z, align_bytes=64)
            spans = [(0, Q)] if z == 0 else [(0, Q // 2), (Q // 2, Q)]
            for lo, hi in spans:
                nc.scalar.copy(
                    grouped[:, lo:hi, :].rearrange("p (c i) t -> p c t i", i=4),
                    hid_rows[z][:, :, lo:hi].rearrange("p t (c i) -> p c t i", i=4),
                )
            hid_codes = keep.tile([P, Q], U32, name="hid_codes%d" % z, align_bytes=64)
            hid_plane = keep.tile([P, Q], U8, name="hid_plane%d" % z, align_bytes=64)
            pieces = [(0, I)] if z == 0 else [(0, HALF), (HALF, HALF)]
            node_words = []
            for n, (start, width) in enumerate(pieces):
                tag = "held1" if n == 1 else "words%d" % z
                words = keep.tile([P, width], U16, name="node_words%d_%d" % (z, n), tag=tag, align_bytes=64)
                nc.vector.tensor_copy(
                    words[:],
                    word_tables[z][:].indirect(node_list[:, start // LIST_ROWS : (start + width) // LIST_ROWS]),
                )
                node_words.append(words)
                if n == 0:
                    for lo, hi in spans:
                        nc.vector.quantize_mx(
                            out=hid_codes[:, lo:hi].bitcast(FP8X4),
                            scales=hid_plane[:, lo:hi],
                            in_=grouped[:, lo:hi, :].rearrange("p q t -> p (q t)"),
                        )
            operands.append((hid_codes, hid_plane, pieces, node_words))

        def multiply(z, c):
            hid_codes, hid_plane, pieces, node_words = operands[z]
            start, width = chunks[c]
            n = 0 if z == 0 else start // HALF
            local = start - pieces[n][0]
            nc.tensor.matmul_mx(
                out=banks[c][:],
                lhsT=hid_codes[:].bitcast(FP8X4),
                lhsT_scale=hid_plane[:],
                rhs=node_words[n][:, local : local + width].bitcast(FP4X4),
                rhs_scale=node_planes[:, z * I + start : z * I + start + width],
                start=(z == 0),
                stop=(z == PASSES - 1),
            )

        for z in range(PASSES):
            multiply(z, 0)
        for z in range(PASSES):
            for c in range(1, len(chunks)):
                multiply(z, c)

        lse_turned = keep.tile([P, 32], F32, name="lse_turned", tag="held0", align_bytes=64)
        nc.vector.transpose(lse_turned[:], lse_rows[:])
        lse_col = lse_turned[:, 0:1]
        neg_lse = keep.tile([P, 1], F32, name="neg_lse", tag="grouped1", align_bytes=64)
        nc.scalar.activation(neg_lse[:], lse_col, ACT.Identity, scale=-1.0)
        for c, (start, width) in enumerate(chunks):
            if c % 2 == 0:
                nc.scalar.activation(logp[:, start : start + width], banks[c][:], ACT.Identity, bias=neg_lse[:])
            else:
                nc.vector.tensor_scalar(logp[:, start : start + width], banks[c][:], lse_col, None, ALU.subtract)

        def listed(s, start, width):
            return logp[:].indirect(step_lists[s][:, start // LIST_ROWS : (start + width) // LIST_ROWS])

        def fresh(name, width):
            return keep.tile([Q, width], F32, name=name, align_bytes=64)

        W = J // 2
        N = W // 2
        y1, y2, y3 = fresh("y1", W), fresh("y2", W), fresh("y3", W)
        x1a, x1b, x2, x3 = fresh("x1a", N), fresh("x1b", N), fresh("x2", W), fresh("x3", W)
        out_a, out_b = fresh("out_a", W), fresh("out_b", W)
        nc.scalar.activation(y1[:], listed(0, W, W), ACT.Copy)
        nc.scalar.activation(y2[:], listed(0, 0, W), ACT.Copy)
        nc.scalar.activation(y3[:, 0:N], listed(1, W, N), ACT.Copy)
        nc.scalar.activation(y3[:, N:W], listed(1, W + N, N), ACT.Copy)
        nc.vector.tensor_copy(x1a[:], listed(2, 0, N))
        nc.vector.tensor_copy(x1b[:], listed(2, N, N))
        nc.vector.tensor_tensor(x2[:, 0:N], listed(1, 0, N), x1a[:], ALU.add)
        nc.vector.tensor_tensor(x2[:, N:W], listed(1, N, N), x1b[:], ALU.add)
        nc.vector.tensor_tensor(x3[:], listed(2, W, W), y1[:], ALU.add)
        nc.vector.tensor_tensor(out_a[:], x2[:], y2[:], ALU.add)
        nc.vector.tensor_tensor(out_b[:, 0:N], x3[:, 0:N], y3[:, 0:N], ALU.add)
        nc.vector.tensor_tensor(out_b[:, N:W], x3[:, N:W], y3[:, N:W], ALU.add)
        nc.sync.dma_start(out[:, 0:W], out_a[:])
        nc.sync.dma_start(out[:, W:J], out_b[:])
